import numpy as np
import ml_dtypes


def mxq(x, axis, fmt="e4m3"):
    dtype, down = {"e4m3": (ml_dtypes.float8_e4m3fn, 7), "e5m2": (ml_dtypes.float8_e5m2, 14)}[fmt]
    v = np.moveaxis(np.asarray(x, np.float32).astype(ml_dtypes.bfloat16).astype(np.float64), axis, -1)
    blocks = v.reshape(v.shape[:-1] + (-1, 32))
    amax = np.abs(blocks).max(-1, keepdims=True)
    byte = np.maximum(np.where(amax > 0, np.frexp(amax)[1] - 1 + 127, 0) - down, 1)
    scale = np.exp2(byte - 127.0)
    codes = (blocks / scale).astype(np.float32).astype(dtype).astype(np.float64)
    return np.moveaxis((codes * scale).reshape(v.shape), -1, axis)


WIDE = False


def mx_kscale(k):
    if not WIDE:
        return np.ones(k)
    levels = np.array([10, -10, 5, -5, 0])
    if k % 512:
        return np.exp2(np.random.permutation(np.resize(levels, k // 32))).repeat(32)
    a = np.empty((k // 512, 16))
    for p in range(k // 512):
        a[p, :8] = np.random.permutation(np.resize(levels, 8))
        for g in range(8):
            far = levels[np.abs(levels - a[p, g]) >= 10]
            a[p, g + 8] = far[np.random.randint(len(far))]
    return np.exp2(a.ravel()).repeat(32)


def f64(x):
    return np.asarray(x).astype(np.float64)


def striped(idx):
    return np.tile(np.asarray(idx).reshape(-1, 16).T, (8, 1)).astype(np.uint16)


def unstriped(offs):
    return offs[:16].T.reshape(-1).astype(np.int64)


def striped8(idx):
    return np.asarray(idx).reshape(8, -1, 16).transpose(0, 2, 1).reshape(128, -1).astype(np.uint16)


def unstriped8(offs):
    return offs.reshape(8, 16, -1).transpose(0, 2, 1).reshape(8, -1).astype(np.int64)


def pick8(x, idx, run):
    r = np.arange(len(x))
    return x[r[:, None], idx[r % (8 * run) // run]]


E2M1 = np.array([0.0, 0.5, 1.0, 1.5, 2.0, 3.0, 4.0, 6.0, -0.0, -0.5, -1.0, -1.5, -2.0, -3.0, -4.0, -6.0])


def pack_weight(w, fmt):
    k, n = w.shape
    w = f64(np.asarray(w, np.float32).astype(ml_dtypes.bfloat16)).reshape(k // 32, 32, n)
    amax = np.abs(w).max(1)
    if fmt == "e4m3":
        byte = np.frexp(amax)[1] - 1 + 127 - 7
    else:
        mant, ex = np.frexp(amax / 6.0)
        byte = np.where(mant > 0.5, ex, ex - 1) + 127
    byte = np.clip(np.where(amax > 0, byte, 1), 1, 254)
    scaled = (w * np.exp2(127.0 - byte)[:, None, :]).reshape(k, n).astype(np.float32)
    by_word = np.ascontiguousarray(scaled.reshape(k // 512, 128, 4, n).transpose(0, 1, 3, 2))
    if fmt == "e4m3":
        words = by_word.astype(ml_dtypes.float8_e4m3fn).view(np.uint8)
    else:
        c = by_word.astype(ml_dtypes.float4_e2m1fn).view(np.uint8) & 0xF
        words = (c[..., 0::2] | (c[..., 1::2] << 4)).reshape(k // 512, 128, 2 * n)
    return np.ascontiguousarray(words), np.ascontiguousarray(byte.astype(np.uint8).reshape(k // 512, 16, n))


def unpack_weight(words, scales, fmt):
    g, _, n = scales.shape
    words = np.ascontiguousarray(words).reshape(g, 128, n, -1)
    if fmt == "e4m3":
        vals = words.view(ml_dtypes.float8_e4m3fn).astype(np.float64)
    else:
        nib = np.empty((g, 128, n, 4), np.uint8)
        nib[..., 0::2] = words & 0xF
        nib[..., 1::2] = words >> 4
        vals = E2M1[nib]
    vals = vals * np.repeat(np.exp2(scales.astype(np.float64) - 127.0), 8, axis=1)[..., None]
    return vals.transpose(0, 1, 3, 2).reshape(g * 512, n)


K, T, S, J, N = 1024, 1024, 512, 512, 512


def setup_inputs():
    n = np.random.standard_normal
    idx = np.stack([np.random.permutation(T)[:J] for _ in range(8)])
    idx2 = np.random.randint(0, S, J)
    fk = mx_kscale(K)
    wp = pack_weight(n((K, N)) * 1 / np.sqrt(K) * fk[:, None], "e2m1")
    return {
        "xf": (n((K, T))).astype(np.float32),
        "tb": (n((K, S))).astype(np.float32),
        "fk": (np.random.uniform(0.5, 2.0, (K, 1)) / fk[:, None]).astype(np.float32),
        "w_words": wp[0],
        "w_scales": wp[1],
        "rw": (np.random.uniform(0.5, 2.0, (1, J))).astype(np.float32),
        "offs": striped8(idx),
        "offs2": striped(idx2),
    }


def reference(xf, tb, fk, w_words, w_scales, rw, offs, offs2):
    idx = unstriped8(offs)
    idx2 = unstriped(offs2)
    wu = unpack_weight(w_words, w_scales, "e2m1")
    u = pick8(f64(xf), idx, 64) * f64(tb)[:, idx2] * f64(fk)
    uq = mxq(u, 0, "e4m3")
    p = wu.T @ uq
    y = p * f64(rw)
    return y

@@ -1,0 +1,168 @@
+from contextlib import ExitStack
+
+import concourse.mybir as mybir
+
+K, T, S, J, N = 1024, 1024, 512, 512, 512
+FLOPS = 2 * K * N * J
+
+F32 = mybir.dt.float32
+BF16 = mybir.dt.bfloat16
+I32 = mybir.dt.int32
+U32 = mybir.dt.uint32
+U16 = mybir.dt.uint16
+U8 = mybir.dt.uint8
+FP8X4 = mybir.dt.float8_e4m3fn_x4
+FP4X4 = mybir.dt.float4_e2m1fn_x4
+MULT = mybir.AluOpType.mult
+COPY = mybir.ActivationFunctionType.Copy
+
+P = 128
+PACK = 4
+PASSES = K // (P * PACK)
+PLANES = PASSES * PACK
+KEY_WINDOW = S + 8
+CHUNK = 128
+CHUNKS = J // CHUNK
+EARLY = J - CHUNK
+TILES = N // P
+
+
+def tile_moe_expert_heads_times_key_kernel(tc, xf, tb, fk, w_words, w_scales, rw, offs, offs2, out):
+    nc = tc.nc
+    with ExitStack() as ctx:
+        keep = ctx.enter_context(tc.tile_pool(name="keep", bufs=1))
+        psum = ctx.enter_context(tc.psum_pool(name="psum", bufs=1))
+
+        token_list = keep.tile([P, J // 16], U16, name="token_list")
+        key_list = keep.tile([P, J // 16], U16, name="key_list")
+        keys = [keep.tile([P, KEY_WINDOW if i < PACK else S], F32, name="keys%d" % i) for i in range(PLANES)]
+        tokens = [keep.tile([P, T], F32, name="tokens%d" % i) for i in range(PLANES)]
+        factors = keep.tile([P, PASSES, PACK], F32, name="factors")
+        spread = [keep.tile([P, J if i < PACK else EARLY], F32, name="spread%d" % i) for i in range(PLANES)]
+        words = keep.tile([P, PASSES, 2 * N], U8, name="words", align_bytes=64)
+        w_plane = keep.tile([P, PASSES, N], U8, name="w_plane", align_bytes=64)
+        router = keep.tile([P, J], F32, name="router")
+
+        xf_planes = xf.rearrange("(z p t) c -> z t p c", z=PASSES, t=PACK)
+        tb_planes = tb.rearrange("(z p t) c -> z t p c", z=PASSES, t=PACK)
+
+        def load_keys(i):
+            nc.sync.dma_start(keys[i][:, 0:S], tb_planes[i // PACK, i % PACK])
+
+        def load_tokens(i):
+            nc.sync.dma_start(tokens[i][:], xf_planes[i // PACK, i % PACK])
+
+        for i in range(PACK):
+            nc.vector.memset(keys[i][:, S:], 0.0)
+        nc.vector.memset(w_plane[:].rearrange("p z n -> p (z n)").bitcast(I32), 0)
+
+        nc.scalar.dma_start(factors[:], fk.rearrange("(z p t) o -> p z (t o)", z=PASSES, t=PACK))
+        nc.sync.dma_start(key_list[:], offs2)
+        load_keys(0)
+        nc.sync.dma_start(token_list[:], offs)
+        load_keys(1)
+        for i in range(PLANES):
+            load_tokens(i)
+            if i + 2 < PLANES:
+                load_keys(i + 2)
+        nc.sync.dma_start(words[:].bitcast(I32), w_words.rearrange("z p b -> p z b").bitcast(I32))
+        for r in range(4):
+            nc.sync.dma_start(
+                w_plane[r:P:32, :, :].bitcast(I32),
+                w_scales.rearrange("z (q r) n -> r q z n", r=4)[r].bitcast(I32),
+            )
+        nc.sync.dma_start(router[:], rw[0].partition_broadcast(P))
+
+        for i in range(PLANES):
+            z, t = divmod(i, PACK)
+            nc.scalar.copy(spread[i][:], factors[:, z, t : t + 1].to_broadcast([P, spread[i].shape[1]]))
+
+        shared = keep.tile([P, PACK * J], F32, name="shared")
+        picked = [shared if r == 1 else keep.tile([P, J], F32, name="picked%d" % r) for r in range(3)]
+        first = keep.tile([P, PACK, J], F32, name="first")
+        early = shared[:, J:].rearrange("p (t j) -> p t j", t=PACK)
+        late = shared[:].rearrange("p (t j) -> p t j", t=PACK)[:, :, 0:CHUNK]
+        grouped = [keep.tile([P, J, PACK], BF16, name="grouped%d" % z, align_bytes=64) for z in range(PASSES)]
+        codes = [keep.tile([P, J], U32, name="codes%d" % z, align_bytes=64) for z in range(PASSES)]
+        u_plane = [keep.tile([P, J], U8, name="u_plane%d" % z, align_bytes=64) for z in range(PASSES)]
+        banks = [psum.tile([P, TILES, CHUNK], F32, name="bank%d" % c) for c in range(CHUNKS - 1)]
+        last_banks = [psum.tile([P, CHUNK], F32, name="last_bank%d" % m) for m in range(TILES)]
+        result = [keep.tile([P, TILES, CHUNK], F32, name="result%d" % c) for c in range(CHUNKS)]
+        out_tiles = out.rearrange("(m p) j -> p m j", p=P)
+
+        steps = [(i, 0, J, first) for i in range(PACK)]
+        steps = steps + [(i, 0, EARLY, early) for i in range(PACK, PLANES)]
+        steps = steps + [(i, EARLY, J, late) for i in range(PACK, PLANES)]
+
+        def staged(s):
+            i, a, b, product = steps[s]
+            start = CHUNK if s >= PLANES else 0
+            return picked[s % 3][:, start : start + b - a]
+
+        def gather_keys(s):
+            i, a, b, product = steps[s]
+            nc.vector.tensor_tensor(
+                staged(s),
+                keys[i][:].indirect(key_list[:, a // 16 : b // 16]),
+                spread[i][:, 0 : b - a],
+                MULT,
+            )
+
+        def gather_tokens(s):
+            i, a, b, product = steps[s]
+            nc.vector.tensor_tensor(
+                product[:, i % PACK, :],
+                tokens[i][:].indirect(token_list[:, a // 16 : b // 16]),
+                staged(s),
+                MULT,
+            )
+
+        def quantize(z, a, b, product):
+            nc.scalar.copy(
+                grouped[z][:, a:b, :].rearrange("p (c i) t -> p c t i", i=4),
+                product.rearrange("p t (c i) -> p c t i", i=4),
+            )
+            nc.vector.quantize_mx(
+                out=codes[z][:, a:b].bitcast(FP8X4),
+                scales=u_plane[z][:, a:b],
+                in_=grouped[z][:, a:b, :].rearrange("p j t -> p (j t)"),
+            )
+
+        def contract(acc, z, m, c):
+            cols = slice(CHUNK * c, CHUNK * (c + 1))
+            nc.tensor.matmul_mx(
+                out=acc,
+                lhsT=words[:, z, 2 * P * m : 2 * P * (m + 1)].bitcast(FP4X4),
+                lhsT_scale=w_plane[:, z, P * m : P * (m + 1)],
+                rhs=codes[z][:, cols].bitcast(FP8X4),
+                rhs_scale=u_plane[z][:, cols],
+                start=(z == 0),
+                stop=(z == PASSES - 1),
+            )
+
+        gather_keys(0)
+        for s in range(len(steps)):
+            if s + 1 < len(steps):
+                gather_keys(s + 1)
+            gather_tokens(s)
+            if s == PACK - 1:
+                quantize(0, 0, J, first[:])
+                for m in range(TILES):
+                    contract(last_banks[m][:], 0, m, CHUNKS - 1)
+            if s == PLANES - 1:
+                for c in range(CHUNKS - 1):
+                    cols = slice(CHUNK * c, CHUNK * (c + 1))
+                    quantize(1, cols.start, cols.stop, early[:, :, cols])
+                    for m in range(TILES):
+                        for z in range(PASSES):
+                            contract(banks[c][:, m, :], z, m, c)
+        quantize(1, EARLY, J, late)
+        for c in range(CHUNKS - 1):
+            cols = slice(CHUNK * c, CHUNK * (c + 1))
+            weight = router[:, cols].unsqueeze(1).to_broadcast([P, TILES, CHUNK])
+            nc.vector.tensor_tensor(result[c][:], banks[c][:], weight, MULT)
+            nc.sync.dma_start(out_tiles[:, :, cols], result[c][:])
+        for m in range(TILES):
+            contract(last_banks[m][:], 1, m, CHUNKS - 1)
+            nc.vector.tensor_tensor(result[CHUNKS - 1][:, m, :], last_banks[m][:], router[:, EARLY:], MULT)
+            nc.sync.dma_start(out_tiles[:, m, EARLY:], result[CHUNKS - 1][:, m, :])

@@ -1,6 +1,7 @@
 from contextlib import ExitStack
 
 import concourse.mybir as mybir
+from concourse.masks import make_identity
 
 K, T, S, J, N = 1024, 1024, 512, 512, 512
 FLOPS = 2 * K * N * J
@@ -23,8 +24,10 @@ PLANES = PASSES * PACK
 KEY_WINDOW = S + 8
 CHUNK = 128
 CHUNKS = J // CHUNK
-EARLY = J - CHUNK
+TURNED = 2
+EARLY = TURNED * CHUNK
 TILES = N // P
+LAST, FIRST, SECOND = 0, 1, 3
 
 
 def tile_moe_expert_heads_times_key_kernel(tc, xf, tb, fk, w_words, w_scales, rw, offs, offs2, out):
@@ -35,13 +38,16 @@ def tile_moe_expert_heads_times_key_kernel(tc, xf, tb, fk, w_words, w_scales, rw
 
         token_list = keep.tile([P, J // 16], U16, name="token_list")
         key_list = keep.tile([P, J // 16], U16, name="key_list")
-        keys = [keep.tile([P, KEY_WINDOW if i < PACK else S], F32, name="keys%d" % i) for i in range(PLANES)]
+        keys = [keep.tile([P, KEY_WINDOW], F32, name="keys%d" % i) for i in range(PLANES)]
         tokens = [keep.tile([P, T], F32, name="tokens%d" % i) for i in range(PLANES)]
         factors = keep.tile([P, PASSES, PACK], F32, name="factors")
-        spread = [keep.tile([P, J if i < PACK else EARLY], F32, name="spread%d" % i) for i in range(PLANES)]
+        spread = [keep.tile([P, J], F32, name="spread%d" % i) for i in range(PLANES)]
         words = keep.tile([P, PASSES, 2 * N], U8, name="words", align_bytes=64)
         w_plane = keep.tile([P, PASSES, N], U8, name="w_plane", align_bytes=64)
-        router = keep.tile([P, J], F32, name="router")
+        router = keep.tile([P, 2, CHUNK], F32, name="router")
+        router_rows = keep.tile([P, TURNED], F32, name="router_rows")
+        identity = keep.tile([P, P], F32, name="identity")
+        make_identity(nc, identity[:])
 
         xf_planes = xf.rearrange("(z p t) c -> z t p c", z=PASSES, t=PACK)
         tb_planes = tb.rearrange("(z p t) c -> z t p c", z=PASSES, t=PACK)
@@ -52,7 +58,7 @@ def tile_moe_expert_heads_times_key_kernel(tc, xf, tb, fk, w_words, w_scales, rw
         def load_tokens(i):
             nc.sync.dma_start(tokens[i][:], xf_planes[i // PACK, i % PACK])
 
-        for i in range(PACK):
+        for i in range(PLANES):
             nc.vector.memset(keys[i][:, S:], 0.0)
         nc.vector.memset(w_plane[:].rearrange("p z n -> p (z n)").bitcast(I32), 0)
 
@@ -61,59 +67,55 @@ def tile_moe_expert_heads_times_key_kernel(tc, xf, tb, fk, w_words, w_scales, rw
         load_keys(0)
         nc.sync.dma_start(token_list[:], offs)
         load_keys(1)
-        for i in range(PLANES):
+        for i in range(PLANES - 2):
             load_tokens(i)
-            if i + 2 < PLANES:
-                load_keys(i + 2)
+            load_keys(i + 2)
         nc.sync.dma_start(words[:].bitcast(I32), w_words.rearrange("z p b -> p z b").bitcast(I32))
         for r in range(4):
             nc.sync.dma_start(
                 w_plane[r:P:32, :, :].bitcast(I32),
                 w_scales.rearrange("z (q r) n -> r q z n", r=4)[r].bitcast(I32),
             )
-        nc.sync.dma_start(router[:], rw[0].partition_broadcast(P))
+        with nc.allow_non_contiguous_dma(reason="one router weight a partition"):
+            nc.sync.dma_start(router_rows[:], rw[0, CHUNK : CHUNK + EARLY].rearrange("(c p) -> p c", p=P))
+        for n, c in enumerate((SECOND, LAST)):
+            nc.sync.dma_start(router[:, n, :], rw[0, CHUNK * c : CHUNK * (c + 1)].partition_broadcast(P))
+        for i in range(PLANES - 2, PLANES):
+            load_tokens(i)
 
         for i in range(PLANES):
             z, t = divmod(i, PACK)
-            nc.scalar.copy(spread[i][:], factors[:, z, t : t + 1].to_broadcast([P, spread[i].shape[1]]))
+            column = factors[:, z, t : t + 1].to_broadcast([P, spread[i].shape[1]])
+            if i == 0:
+                nc.vector.tensor_copy(spread[i][:], column)
+            else:
+                nc.scalar.copy(spread[i][:], column)
 
         shared = keep.tile([P, PACK * J], F32, name="shared")
-        picked = [shared if r == 1 else keep.tile([P, J], F32, name="picked%d" % r) for r in range(3)]
-        first = keep.tile([P, PACK, J], F32, name="first")
-        early = shared[:, J:].rearrange("p (t j) -> p t j", t=PACK)
-        late = shared[:].rearrange("p (t j) -> p t j", t=PACK)[:, :, 0:CHUNK]
+        picked = [keep.tile([P, J], F32, name="picked%d" % t)[:] for t in range(2)]
+        picked = picked + [shared[:, 0:J], shared[:, 3 * J :]]
+        whole = keep.tile([P, PACK, J], F32, name="whole")
+        first = shared[:, J : 3 * J].rearrange("p (t j) -> p t j", t=PACK)
+        second = shared[:, 3 * CHUNK : 15 * CHUNK].rearrange("p (t j) -> p t j", t=PACK)[:, :, 2 * CHUNK :]
+        last = shared[:, 320 : 320 + J].rearrange("p (t j) -> p t j", t=PACK)
         grouped = [keep.tile([P, J, PACK], BF16, name="grouped%d" % z, align_bytes=64) for z in range(PASSES)]
         codes = [keep.tile([P, J], U32, name="codes%d" % z, align_bytes=64) for z in range(PASSES)]
         u_plane = [keep.tile([P, J], U8, name="u_plane%d" % z, align_bytes=64) for z in range(PASSES)]
-        banks = [psum.tile([P, TILES, CHUNK], F32, name="bank%d" % c) for c in range(CHUNKS - 1)]
+        by_slot = [psum.tile([P, N], F32, name="by_slot%d" % c, tag="turned%d" % c) for c in range(TURNED)]
+        bank = psum.tile([P, TILES, CHUNK], F32, name="bank")
         last_banks = [psum.tile([P, CHUNK], F32, name="last_bank%d" % m) for m in range(TILES)]
+        scaled = [keep.tile([P, N], F32, name="scaled%d" % c) for c in range(TURNED)]
         result = [keep.tile([P, TILES, CHUNK], F32, name="result%d" % c) for c in range(CHUNKS)]
         out_tiles = out.rearrange("(m p) j -> p m j", p=P)
 
-        steps = [(i, 0, J, first) for i in range(PACK)]
-        steps = steps + [(i, 0, EARLY, early) for i in range(PACK, PLANES)]
-        steps = steps + [(i, EARLY, J, late) for i in range(PACK, PLANES)]
+        def gather_keys(i):
+            nc.vector.tensor_tensor(picked[i % PACK], keys[i][:].indirect(key_list[:]), spread[i][:], MULT)
 
-        def staged(s):
-            i, a, b, product = steps[s]
-            start = CHUNK if s >= PLANES else 0
-            return picked[s % 3][:, start : start + b - a]
-
-        def gather_keys(s):
-            i, a, b, product = steps[s]
+        def gather_tokens(i, a, b, product):
             nc.vector.tensor_tensor(
-                staged(s),
-                keys[i][:].indirect(key_list[:, a // 16 : b // 16]),
-                spread[i][:, 0 : b - a],
-                MULT,
-            )
-
-        def gather_tokens(s):
-            i, a, b, product = steps[s]
-            nc.vector.tensor_tensor(
-                product[:, i % PACK, :],
+                product,
                 tokens[i][:].indirect(token_list[:, a // 16 : b // 16]),
-                staged(s),
+                picked[i % PACK][:, a:b],
                 MULT,
             )
 
@@ -140,29 +142,77 @@ def tile_moe_expert_heads_times_key_kernel(tc, xf, tb, fk, w_words, w_scales, rw
                 stop=(z == PASSES - 1),
             )
 
+        def contract_by_slot(z, h):
+            cols = slice(CHUNK * (FIRST + h), CHUNK * (FIRST + h + 1))
+            nc.tensor.matmul_mx(
+                out=by_slot[h][:],
+                lhsT=codes[z][:, cols].bitcast(FP8X4),
+                lhsT_scale=u_plane[z][:, cols],
+                rhs=words[:, z, :].bitcast(FP4X4),
+                rhs_scale=w_plane[:, z, :],
+                start=(z == 0),
+                stop=(z == PASSES - 1),
+            )
+
+        def weigh_and_turn(h):
+            nc.scalar.activation(scaled[h][:], by_slot[h][:], COPY, scale=router_rows[:, h : h + 1])
+            turned = psum.tile([P, TILES, CHUNK], F32, name="turned%d" % h, tag="turned%d" % h)
+            for m in range(TILES):
+                nc.tensor.transpose(turned[:, m, :], scaled[h][:, P * m : P * (m + 1)], identity[:])
+            return turned
+
+        def store_turned(h, turned):
+            c = FIRST + h
+            nc.scalar.copy(result[c][:], turned[:])
+            nc.sync.dma_start(out_tiles[:, :, CHUNK * c : CHUNK * (c + 1)], result[c][:])
+
+        def gather_chunk(t, c, product):
+            gather_tokens(PACK + t, CHUNK * c, CHUNK * (c + 1), product[:, t, :])
+
+        def quantize_chunk(c, product):
+            quantize(1, CHUNK * c, CHUNK * (c + 1), product)
+
         gather_keys(0)
-        for s in range(len(steps)):
-            if s + 1 < len(steps):
-                gather_keys(s + 1)
-            gather_tokens(s)
-            if s == PACK - 1:
-                quantize(0, 0, J, first[:])
+        for i in range(PLANES - 1):
+            gather_keys(i + 1)
+            if i < PACK:
+                gather_tokens(i, 0, J, whole[:, i, :])
+            else:
+                gather_tokens(i, CHUNK * FIRST, CHUNK * FIRST + EARLY, first[:, i - PACK, :])
+            if i == PACK - 1:
+                quantize(0, 0, J, whole[:])
+                for h in range(TURNED):
+                    contract_by_slot(0, h)
                 for m in range(TILES):
-                    contract(last_banks[m][:], 0, m, CHUNKS - 1)
-            if s == PLANES - 1:
-                for c in range(CHUNKS - 1):
-                    cols = slice(CHUNK * c, CHUNK * (c + 1))
-                    quantize(1, cols.start, cols.stop, early[:, :, cols])
-                    for m in range(TILES):
-                        for z in range(PASSES):
-                            contract(banks[c][:, m, :], z, m, c)
-        quantize(1, EARLY, J, late)
-        for c in range(CHUNKS - 1):
-            cols = slice(CHUNK * c, CHUNK * (c + 1))
-            weight = router[:, cols].unsqueeze(1).to_broadcast([P, TILES, CHUNK])
-            nc.vector.tensor_tensor(result[c][:], banks[c][:], weight, MULT)
-            nc.sync.dma_start(out_tiles[:, :, cols], result[c][:])
+                    contract(last_banks[m][:], 0, m, LAST)
+        halves = [first[:, :, CHUNK * h : CHUNK * (h + 1)] for h in range(TURNED)]
+        for h in range(TURNED):
+            gather_chunk(PACK - 1, FIRST + h, halves[h])
+        gather_chunk(3, SECOND, second)
+        quantize_chunk(FIRST, halves[0])
+        contract_by_slot(1, 0)
+        gather_chunk(1, SECOND, second)
+        quantize_chunk(FIRST + 1, halves[1])
+        contract_by_slot(1, 1)
+        turned0 = weigh_and_turn(0)
+        gather_chunk(0, SECOND, second)
+        gather_chunk(2, SECOND, second)
+        gather_chunk(0, LAST, last)
+        gather_chunk(1, LAST, last)
+        quantize_chunk(SECOND, second)
         for m in range(TILES):
-            contract(last_banks[m][:], 1, m, CHUNKS - 1)
-            nc.vector.tensor_tensor(result[CHUNKS - 1][:, m, :], last_banks[m][:], router[:, EARLY:], MULT)
-            nc.sync.dma_start(out_tiles[:, m, EARLY:], result[CHUNKS - 1][:, m, :])
+            for z in range(PASSES):
+                contract(bank[:, m, :], z, m, SECOND)
+        gather_chunk(2, LAST, last)
+        gather_chunk(3, LAST, last)
+        turned1 = weigh_and_turn(1)
+        store_turned(0, turned0)
+        weight = router[:, 0, :].unsqueeze(1).to_broadcast([P, TILES, CHUNK])
+        nc.vector.tensor_tensor(result[SECOND][:], bank[:], weight, MULT)
+        nc.sync.dma_start(out_tiles[:, :, CHUNK * SECOND : CHUNK * (SECOND + 1)], result[SECOND][:])
+        quantize_chunk(LAST, last)
+        store_turned(1, turned1)
+        for m in range(TILES):
+            contract(last_banks[m][:], 1, m, LAST)
+            nc.vector.tensor_tensor(result[LAST][:, m, :], last_banks[m][:], router[:, 1, :], MULT)
+            nc.sync.dma_start(out_tiles[:, m, CHUNK * LAST : CHUNK * (LAST + 1)], result[LAST][:, m, :])

@@ -21,7 +21,7 @@ P = 128
 PACK = 4
 PASSES = K // (P * PACK)
 PLANES = PASSES * PACK
-KEY_WINDOW = S + 8
+KEY_WINDOW = 704
 CHUNK = 128
 CHUNKS = J // CHUNK
 TURNED = 2
@@ -38,58 +38,60 @@ def tile_moe_expert_heads_times_key_kernel(tc, xf, tb, fk, w_words, w_scales, rw
 
         token_list = keep.tile([P, J // 16], U16, name="token_list")
         key_list = keep.tile([P, J // 16], U16, name="key_list")
-        keys = [keep.tile([P, KEY_WINDOW], F32, name="keys%d" % i) for i in range(PLANES)]
+        keys = keep.tile([P, PLANES * S + KEY_WINDOW - S], F32, name="keys")
         tokens = [keep.tile([P, T], F32, name="tokens%d" % i) for i in range(PLANES)]
         factors = keep.tile([P, PASSES, PACK], F32, name="factors")
-        spread = [keep.tile([P, J], F32, name="spread%d" % i) for i in range(PLANES)]
         words = keep.tile([P, PASSES, 2 * N], U8, name="words", align_bytes=64)
         w_plane = keep.tile([P, PASSES, N], U8, name="w_plane", align_bytes=64)
         router = keep.tile([P, 2, CHUNK], F32, name="router")
-        router_rows = keep.tile([P, TURNED], F32, name="router_rows")
+        router_rows = keep.tile([P, CHUNKS], F32, name="router_rows")
+        router_raw = keep.tile([P, CHUNK], F32, name="router_raw")
+        nc.gpsimd.memset(router_raw[:], 0.0)
         identity = keep.tile([P, P], F32, name="identity")
         make_identity(nc, identity[:])
 
         xf_planes = xf.rearrange("(z p t) c -> z t p c", z=PASSES, t=PACK)
         tb_planes = tb.rearrange("(z p t) c -> z t p c", z=PASSES, t=PACK)
 
+        def key_start(i):
+            return (PLANES - 1 - i) * S
+
         def load_keys(i):
-            nc.sync.dma_start(keys[i][:, 0:S], tb_planes[i // PACK, i % PACK])
+            nc.sync.dma_start(keys[:, key_start(i) : key_start(i) + S], tb_planes[i // PACK, i % PACK])
 
         def load_tokens(i):
             nc.sync.dma_start(tokens[i][:], xf_planes[i // PACK, i % PACK])
 
-        for i in range(PLANES):
-            nc.vector.memset(keys[i][:, S:], 0.0)
+        nc.vector.memset(keys[:, PLANES * S :], 0.0)
         nc.vector.memset(w_plane[:].rearrange("p z n -> p (z n)").bitcast(I32), 0)
 
         nc.scalar.dma_start(factors[:], fk.rearrange("(z p t) o -> p z (t o)", z=PASSES, t=PACK))
+        nc.scalar.dma_start(router_raw[0:CHUNKS, :], rw.rearrange("o (c j) -> (o c) j", c=CHUNKS))
         nc.sync.dma_start(key_list[:], offs2)
         load_keys(0)
         nc.sync.dma_start(token_list[:], offs)
         load_keys(1)
-        for i in range(PLANES - 2):
+        for i in range(PLANES - 3):
             load_tokens(i)
             load_keys(i + 2)
+        load_keys(PLANES - 1)
+        load_tokens(PLANES - 3)
         nc.sync.dma_start(words[:].bitcast(I32), w_words.rearrange("z p b -> p z b").bitcast(I32))
         for r in range(4):
             nc.sync.dma_start(
                 w_plane[r:P:32, :, :].bitcast(I32),
                 w_scales.rearrange("z (q r) n -> r q z n", r=4)[r].bitcast(I32),
             )
-        with nc.allow_non_contiguous_dma(reason="one router weight a partition"):
-            nc.sync.dma_start(router_rows[:], rw[0, CHUNK : CHUNK + EARLY].rearrange("(c p) -> p c", p=P))
-        for n, c in enumerate((SECOND, LAST)):
-            nc.sync.dma_start(router[:, n, :], rw[0, CHUNK * c : CHUNK * (c + 1)].partition_broadcast(P))
         for i in range(PLANES - 2, PLANES):
             load_tokens(i)
 
-        for i in range(PLANES):
-            z, t = divmod(i, PACK)
-            column = factors[:, z, t : t + 1].to_broadcast([P, spread[i].shape[1]])
-            if i == 0:
-                nc.vector.tensor_copy(spread[i][:], column)
-            else:
-                nc.scalar.copy(spread[i][:], column)
+        on_rows = psum.tile([P, P], F32, name="on_rows", tag="router")
+        nc.tensor.transpose(on_rows[:], router_raw[:], identity[:])
+        nc.scalar.copy(router_rows[:], on_rows[:, 0:CHUNKS])
+        on_columns = psum.tile([P, 2, CHUNK], F32, name="on_columns", tag="router")
+        for n, c in enumerate((SECOND, LAST)):
+            nc.tensor.transpose(on_columns[:, n, :], router_rows[:, c : c + 1].to_broadcast([P, P]), identity[:])
+        nc.scalar.copy(router[:], on_columns[:])
 
         shared = keep.tile([P, PACK * J], F32, name="shared")
         picked = [keep.tile([P, J], F32, name="picked%d" % t)[:] for t in range(2)]
@@ -109,7 +111,10 @@ def tile_moe_expert_heads_times_key_kernel(tc, xf, tb, fk, w_words, w_scales, rw
         out_tiles = out.rearrange("(m p) j -> p m j", p=P)
 
         def gather_keys(i):
-            nc.vector.tensor_tensor(picked[i % PACK], keys[i][:].indirect(key_list[:]), spread[i][:], MULT)
+            z, t = divmod(i, PACK)
+            window = keys[:, key_start(i) : key_start(i) + KEY_WINDOW]
+            nc.vector.tensor_copy(picked[t], window.indirect(key_list[:]))
+            nc.scalar.activation(picked[t], picked[t], COPY, scale=factors[:, z, t : t + 1])
 
         def gather_tokens(i, a, b, product):
             nc.vector.tensor_tensor(
@@ -155,7 +160,7 @@ def tile_moe_expert_heads_times_key_kernel(tc, xf, tb, fk, w_words, w_scales, rw
             )
 
         def weigh_and_turn(h):
-            nc.scalar.activation(scaled[h][:], by_slot[h][:], COPY, scale=router_rows[:, h : h + 1])
+            nc.scalar.activation(scaled[h][:], by_slot[h][:], COPY, scale=router_rows[:, FIRST + h : FIRST + h + 1])
             turned = psum.tile([P, TILES, CHUNK], F32, name="turned%d" % h, tag="turned%d" % h)
             for m in range(TILES):
                 nc.tensor.transpose(turned[:, m, :], scaled[h][:, P * m : P * (m + 1)], identity[:])
@@ -174,7 +179,10 @@ def tile_moe_expert_heads_times_key_kernel(tc, xf, tb, fk, w_words, w_scales, rw
 
         gather_keys(0)
         for i in range(PLANES - 1):
-            gather_keys(i + 1)
+            if i < PLANES - 2:
+                gather_keys(i + 1)
+            if i == PLANES - 3:
+                gather_keys(i + 2)
             if i < PACK:
                 gather_tokens(i, 0, J, whole[:, i, :])
             else:

@@ -38,12 +38,11 @@ def tile_moe_expert_heads_times_key_kernel(tc, xf, tb, fk, w_words, w_scales, rw
 
         token_list = keep.tile([P, J // 16], U16, name="token_list")
         key_list = keep.tile([P, J // 16], U16, name="key_list")
-        keys = keep.tile([P, PLANES * S + KEY_WINDOW - S], F32, name="keys")
-        tokens = [keep.tile([P, T], F32, name="tokens%d" % i) for i in range(PLANES)]
+        keys = keep.tile([P, PLANES * S + KEY_WINDOW - S], F32, name="keys", align_bytes=256)
+        tokens = [keep.tile([P, T], F32, name="tokens%d" % i, align_bytes=256) for i in range(PLANES)]
         factors = keep.tile([P, PASSES, PACK], F32, name="factors")
-        words = keep.tile([P, PASSES, 2 * N], U8, name="words", align_bytes=64)
+        words = keep.tile([P, PASSES, 2 * N], U8, name="words", align_bytes=256)
         w_plane = keep.tile([P, PASSES, N], U8, name="w_plane", align_bytes=64)
-        router = keep.tile([P, 2, CHUNK], F32, name="router")
         router_rows = keep.tile([P, CHUNKS], F32, name="router_rows")
         router_raw = keep.tile([P, CHUNK], F32, name="router_raw")
         nc.gpsimd.memset(router_raw[:], 0.0)
@@ -66,7 +65,6 @@ def tile_moe_expert_heads_times_key_kernel(tc, xf, tb, fk, w_words, w_scales, rw
         nc.vector.memset(w_plane[:].rearrange("p z n -> p (z n)").bitcast(I32), 0)
 
         nc.scalar.dma_start(factors[:], fk.rearrange("(z p t) o -> p z (t o)", z=PASSES, t=PACK))
-        nc.scalar.dma_start(router_raw[0:CHUNKS, :], rw.rearrange("o (c j) -> (o c) j", c=CHUNKS))
         nc.sync.dma_start(key_list[:], offs2)
         load_keys(0)
         nc.sync.dma_start(token_list[:], offs)
@@ -76,22 +74,24 @@ def tile_moe_expert_heads_times_key_kernel(tc, xf, tb, fk, w_words, w_scales, rw
             load_keys(i + 2)
         load_keys(PLANES - 1)
         load_tokens(PLANES - 3)
+        nc.sync.dma_start(router_raw[0:CHUNKS, :], rw.rearrange("o (c j) -> (o c) j", c=CHUNKS))
+        load_tokens(PLANES - 2)
         nc.sync.dma_start(words[:].bitcast(I32), w_words.rearrange("z p b -> p z b").bitcast(I32))
         for r in range(4):
             nc.sync.dma_start(
                 w_plane[r:P:32, :, :].bitcast(I32),
                 w_scales.rearrange("z (q r) n -> r q z n", r=4)[r].bitcast(I32),
             )
-        for i in range(PLANES - 2, PLANES):
-            load_tokens(i)
+        load_tokens(PLANES - 1)
 
-        on_rows = psum.tile([P, P], F32, name="on_rows", tag="router")
-        nc.tensor.transpose(on_rows[:], router_raw[:], identity[:])
-        nc.scalar.copy(router_rows[:], on_rows[:, 0:CHUNKS])
-        on_columns = psum.tile([P, 2, CHUNK], F32, name="on_columns", tag="router")
-        for n, c in enumerate((SECOND, LAST)):
-            nc.tensor.transpose(on_columns[:, n, :], router_rows[:, c : c + 1].to_broadcast([P, P]), identity[:])
-        nc.scalar.copy(router[:], on_columns[:])
+        def spread_router():
+            on_rows = psum.tile([P, P], F32, name="on_rows", tag="router")
+            nc.tensor.transpose(on_rows[:], router_raw[:], identity[:])
+            nc.scalar.copy(router_rows[:], on_rows[:, 0:CHUNKS])
+            on_columns = psum.tile([P, 2, CHUNK], F32, name="on_columns", tag="router")
+            for n, c in enumerate((SECOND, LAST)):
+                nc.tensor.transpose(on_columns[:, n, :], router_rows[:, c : c + 1].to_broadcast([P, P]), identity[:])
+            return on_columns
 
         shared = keep.tile([P, PACK * J], F32, name="shared")
         picked = [keep.tile([P, J], F32, name="picked%d" % t)[:] for t in range(2)]
@@ -100,6 +100,7 @@ def tile_moe_expert_heads_times_key_kernel(tc, xf, tb, fk, w_words, w_scales, rw
         first = shared[:, J : 3 * J].rearrange("p (t j) -> p t j", t=PACK)
         second = shared[:, 3 * CHUNK : 15 * CHUNK].rearrange("p (t j) -> p t j", t=PACK)[:, :, 2 * CHUNK :]
         last = shared[:, 320 : 320 + J].rearrange("p (t j) -> p t j", t=PACK)
+        router = shared[:, 7 * CHUNK : 11 * CHUNK].rearrange("p (n j) -> p n j", n=2)[:, :, 0:CHUNK]
         grouped = [keep.tile([P, J, PACK], BF16, name="grouped%d" % z, align_bytes=64) for z in range(PASSES)]
         codes = [keep.tile([P, J], U32, name="codes%d" % z, align_bytes=64) for z in range(PASSES)]
         u_plane = [keep.tile([P, J], U8, name="u_plane%d" % z, align_bytes=64) for z in range(PASSES)]
@@ -169,7 +170,8 @@ def tile_moe_expert_heads_times_key_kernel(tc, xf, tb, fk, w_words, w_scales, rw
         def store_turned(h, turned):
             c = FIRST + h
             nc.scalar.copy(result[c][:], turned[:])
-            nc.sync.dma_start(out_tiles[:, :, CHUNK * c : CHUNK * (c + 1)], result[c][:])
+            queue = nc.scalar if h == TURNED - 1 else nc.sync
+            queue.dma_start(out_tiles[:, :, CHUNK * c : CHUNK * (c + 1)], result[c][:])
 
         def gather_chunk(t, c, product):
             gather_tokens(PACK + t, CHUNK * c, CHUNK * (c + 1), product[:, t, :])
@@ -183,6 +185,7 @@ def tile_moe_expert_heads_times_key_kernel(tc, xf, tb, fk, w_words, w_scales, rw
                 gather_keys(i + 1)
             if i == PLANES - 3:
                 gather_keys(i + 2)
+                on_columns = spread_router()
             if i < PACK:
                 gather_tokens(i, 0, J, whole[:, i, :])
             else:
@@ -202,6 +205,7 @@ def tile_moe_expert_heads_times_key_kernel(tc, xf, tb, fk, w_words, w_scales, rw
         gather_chunk(1, SECOND, second)
         quantize_chunk(FIRST + 1, halves[1])
         contract_by_slot(1, 1)
+        nc.scalar.copy(router, on_columns[:])
         turned0 = weigh_and_turn(0)
         gather_chunk(0, SECOND, second)
         gather_chunk(2, SECOND, second)
@@ -223,4 +227,5 @@ def tile_moe_expert_heads_times_key_kernel(tc, xf, tb, fk, w_words, w_scales, rw
         for m in range(TILES):
             contract(last_banks[m][:], 1, m, LAST)
             nc.vector.tensor_tensor(result[LAST][:, m, :], last_banks[m][:], router[:, 1, :], MULT)
-            nc.sync.dma_start(out_tiles[:, m, CHUNK * LAST : CHUNK * (LAST + 1)], result[LAST][:, m, :])
+            queue = nc.scalar if m % 2 else nc.sync
+            queue.dma_start(out_tiles[:, m, CHUNK * LAST : CHUNK * (LAST + 1)], result[LAST][:, m, :])

from contextlib import ExitStack

import concourse.mybir as mybir
from concourse.masks import make_identity

K, T, S, J, N = 1024, 1024, 512, 512, 512
FLOPS = 2 * K * N * J

F32 = mybir.dt.float32
BF16 = mybir.dt.bfloat16
I32 = mybir.dt.int32
U32 = mybir.dt.uint32
U16 = mybir.dt.uint16
U8 = mybir.dt.uint8
FP8X4 = mybir.dt.float8_e4m3fn_x4
FP4X4 = mybir.dt.float4_e2m1fn_x4
MULT = mybir.AluOpType.mult
COPY = mybir.ActivationFunctionType.Copy

P = 128
PACK = 4
PASSES = K // (P * PACK)
PLANES = PASSES * PACK
KEY_WINDOW = 704
CHUNK = 128
CHUNKS = J // CHUNK
TURNED = 2
EARLY = TURNED * CHUNK
TILES = N // P
LAST, FIRST, SECOND = 0, 1, 3


def tile_moe_expert_heads_times_key_kernel(tc, xf, tb, fk, w_words, w_scales, rw, offs, offs2, out):
    nc = tc.nc
    with ExitStack() as ctx:
        keep = ctx.enter_context(tc.tile_pool(name="keep", bufs=1))
        psum = ctx.enter_context(tc.psum_pool(name="psum", bufs=1))

        token_list = keep.tile([P, J // 16], U16, name="token_list")
        key_list = keep.tile([P, J // 16], U16, name="key_list")
        keys = keep.tile([P, PLANES * S + KEY_WINDOW - S], F32, name="keys", align_bytes=256)
        tokens = [keep.tile([P, T], F32, name="tokens%d" % i, align_bytes=256) for i in range(PLANES)]
        factors = keep.tile([P, PASSES, PACK], F32, name="factors")
        words = keep.tile([P, PASSES, 2 * N], U8, name="words", align_bytes=256)
        w_plane = keep.tile([P, PASSES, N], U8, name="w_plane", align_bytes=64)
        router_rows = keep.tile([P, CHUNKS], F32, name="router_rows")
        router_raw = keep.tile([P, CHUNK], F32, name="router_raw")
        nc.gpsimd.memset(router_raw[:], 0.0)
        identity = keep.tile([P, P], F32, name="identity")
        make_identity(nc, identity[:])

        xf_planes = xf.rearrange("(z p t) c -> z t p c", z=PASSES, t=PACK)
        tb_planes = tb.rearrange("(z p t) c -> z t p c", z=PASSES, t=PACK)

        def key_start(i):
            return (PLANES - 1 - i) * S

        def load_keys(i):
            nc.sync.dma_start(keys[:, key_start(i) : key_start(i) + S], tb_planes[i // PACK, i % PACK])

        def load_tokens(i):
            nc.sync.dma_start(tokens[i][:], xf_planes[i // PACK, i % PACK])

        nc.vector.memset(keys[:, PLANES * S :], 0.0)
        nc.vector.memset(w_plane[:].rearrange("p z n -> p (z n)").bitcast(I32), 0)

        nc.scalar.dma_start(factors[:], fk.rearrange("(z p t) o -> p z (t o)", z=PASSES, t=PACK))
        nc.sync.dma_start(key_list[:], offs2)
        load_keys(0)
        nc.sync.dma_start(token_list[:], offs)
        load_keys(1)
        for i in range(PLANES - 3):
            load_tokens(i)
            load_keys(i + 2)
        load_keys(PLANES - 1)
        load_tokens(PLANES - 3)
        nc.sync.dma_start(router_raw[0:CHUNKS, :], rw.rearrange("o (c j) -> (o c) j", c=CHUNKS))
        load_tokens(PLANES - 2)
        nc.sync.dma_start(words[:].bitcast(I32), w_words.rearrange("z p b -> p z b").bitcast(I32))
        for r in range(4):
            nc.sync.dma_start(
                w_plane[r:P:32, :, :].bitcast(I32),
                w_scales.rearrange("z (q r) n -> r q z n", r=4)[r].bitcast(I32),
            )
        load_tokens(PLANES - 1)

        def spread_router():
            on_rows = psum.tile([P, P], F32, name="on_rows", tag="router")
            nc.tensor.transpose(on_rows[:], router_raw[:], identity[:])
            nc.scalar.copy(router_rows[:], on_rows[:, 0:CHUNKS])
            on_columns = psum.tile([P, 2, CHUNK], F32, name="on_columns", tag="router")
            for n, c in enumerate((SECOND, LAST)):
                nc.tensor.transpose(on_columns[:, n, :], router_rows[:, c : c + 1].to_broadcast([P, P]), identity[:])
            return on_columns

        shared = keep.tile([P, PACK * J], F32, name="shared")
        picked = [keep.tile([P, J], F32, name="picked%d" % t)[:] for t in range(2)]
        picked = picked + [shared[:, 0:J], shared[:, 3 * J :]]
        whole = keep.tile([P, PACK, J], F32, name="whole")
        first = shared[:, J : 3 * J].rearrange("p (t j) -> p t j", t=PACK)
        second = shared[:, 3 * CHUNK : 15 * CHUNK].rearrange("p (t j) -> p t j", t=PACK)[:, :, 2 * CHUNK :]
        last = shared[:, 320 : 320 + J].rearrange("p (t j) -> p t j", t=PACK)
        router = shared[:, 7 * CHUNK : 11 * CHUNK].rearrange("p (n j) -> p n j", n=2)[:, :, 0:CHUNK]
        grouped = [keep.tile([P, J, PACK], BF16, name="grouped%d" % z, align_bytes=64) for z in range(PASSES)]
        codes = [keep.tile([P, J], U32, name="codes%d" % z, align_bytes=64) for z in range(PASSES)]
        u_plane = [keep.tile([P, J], U8, name="u_plane%d" % z, align_bytes=64) for z in range(PASSES)]
        by_slot = [psum.tile([P, N], F32, name="by_slot%d" % c, tag="turned%d" % c) for c in range(TURNED)]
        bank = psum.tile([P, TILES, CHUNK], F32, name="bank")
        last_banks = [psum.tile([P, CHUNK], F32, name="last_bank%d" % m) for m in range(TILES)]
        scaled = [keep.tile([P, N], F32, name="scaled%d" % c) for c in range(TURNED)]
        result = [keep.tile([P, TILES, CHUNK], F32, name="result%d" % c) for c in range(CHUNKS)]
        out_tiles = out.rearrange("(m p) j -> p m j", p=P)

        def gather_keys(i):
            z, t = divmod(i, PACK)
            window = keys[:, key_start(i) : key_start(i) + KEY_WINDOW]
            nc.vector.tensor_copy(picked[t], window.indirect(key_list[:]))
            nc.scalar.activation(picked[t], picked[t], COPY, scale=factors[:, z, t : t + 1])

        def gather_tokens(i, a, b, product):
            nc.vector.tensor_tensor(
                product,
                tokens[i][:].indirect(token_list[:, a // 16 : b // 16]),
                picked[i % PACK][:, a:b],
                MULT,
            )

        def quantize(z, a, b, product):
            nc.scalar.copy(
                grouped[z][:, a:b, :].rearrange("p (c i) t -> p c t i", i=4),
                product.rearrange("p t (c i) -> p c t i", i=4),
            )
            nc.vector.quantize_mx(
                out=codes[z][:, a:b].bitcast(FP8X4),
                scales=u_plane[z][:, a:b],
                in_=grouped[z][:, a:b, :].rearrange("p j t -> p (j t)"),
            )

        def contract(acc, z, m, c):
            cols = slice(CHUNK * c, CHUNK * (c + 1))
            nc.tensor.matmul_mx(
                out=acc,
                lhsT=words[:, z, 2 * P * m : 2 * P * (m + 1)].bitcast(FP4X4),
                lhsT_scale=w_plane[:, z, P * m : P * (m + 1)],
                rhs=codes[z][:, cols].bitcast(FP8X4),
                rhs_scale=u_plane[z][:, cols],
                start=(z == 0),
                stop=(z == PASSES - 1),
            )

        def contract_by_slot(z, h):
            cols = slice(CHUNK * (FIRST + h), CHUNK * (FIRST + h + 1))
            nc.tensor.matmul_mx(
                out=by_slot[h][:],
                lhsT=codes[z][:, cols].bitcast(FP8X4),
                lhsT_scale=u_plane[z][:, cols],
                rhs=words[:, z, :].bitcast(FP4X4),
                rhs_scale=w_plane[:, z, :],
                start=(z == 0),
                stop=(z == PASSES - 1),
            )

        def weigh_and_turn(h):
            nc.scalar.activation(scaled[h][:], by_slot[h][:], COPY, scale=router_rows[:, FIRST + h : FIRST + h + 1])
            turned = psum.tile([P, TILES, CHUNK], F32, name="turned%d" % h, tag="turned%d" % h)
            for m in range(TILES):
                nc.tensor.transpose(turned[:, m, :], scaled[h][:, P * m : P * (m + 1)], identity[:])
            return turned

        def store_turned(h, turned):
            c = FIRST + h
            nc.scalar.copy(result[c][:], turned[:])
            queue = nc.scalar if h == TURNED - 1 else nc.sync
            queue.dma_start(out_tiles[:, :, CHUNK * c : CHUNK * (c + 1)], result[c][:])

        def gather_chunk(t, c, product):
            gather_tokens(PACK + t, CHUNK * c, CHUNK * (c + 1), product[:, t, :])

        def quantize_chunk(c, product):
            quantize(1, CHUNK * c, CHUNK * (c + 1), product)

        gather_keys(0)
        for i in range(PLANES - 1):
            if i < PLANES - 2:
                gather_keys(i + 1)
            if i == PLANES - 3:
                gather_keys(i + 2)
                on_columns = spread_router()
            if i < PACK:
                gather_tokens(i, 0, J, whole[:, i, :])
            else:
                gather_tokens(i, CHUNK * FIRST, CHUNK * FIRST + EARLY, first[:, i - PACK, :])
            if i == PACK - 1:
                quantize(0, 0, J, whole[:])
                for h in range(TURNED):
                    contract_by_slot(0, h)
                for m in range(TILES):
                    contract(last_banks[m][:], 0, m, LAST)
        halves = [first[:, :, CHUNK * h : CHUNK * (h + 1)] for h in range(TURNED)]
        for h in range(TURNED):
            gather_chunk(PACK - 1, FIRST + h, halves[h])
        gather_chunk(3, SECOND, second)
        quantize_chunk(FIRST, halves[0])
        contract_by_slot(1, 0)
        gather_chunk(1, SECOND, second)
        quantize_chunk(FIRST + 1, halves[1])
        contract_by_slot(1, 1)
        nc.scalar.copy(router, on_columns[:])
        turned0 = weigh_and_turn(0)
        gather_chunk(0, SECOND, second)
        gather_chunk(2, SECOND, second)
        gather_chunk(0, LAST, last)
        gather_chunk(1, LAST, last)
        quantize_chunk(SECOND, second)
        for m in range(TILES):
            for z in range(PASSES):
                contract(bank[:, m, :], z, m, SECOND)
        gather_chunk(2, LAST, last)
        gather_chunk(3, LAST, last)
        turned1 = weigh_and_turn(1)
        store_turned(0, turned0)
        weight = router[:, 0, :].unsqueeze(1).to_broadcast([P, TILES, CHUNK])
        nc.vector.tensor_tensor(result[SECOND][:], bank[:], weight, MULT)
        nc.sync.dma_start(out_tiles[:, :, CHUNK * SECOND : CHUNK * (SECOND + 1)], result[SECOND][:])
        quantize_chunk(LAST, last)
        store_turned(1, turned1)
        for m in range(TILES):
            contract(last_banks[m][:], 1, m, LAST)
            nc.vector.tensor_tensor(result[LAST][:, m, :], last_banks[m][:], router[:, 1, :], MULT)
            queue = nc.scalar if m % 2 else nc.sync
            queue.dma_start(out_tiles[:, m, CHUNK * LAST : CHUNK * (LAST + 1)], result[LAST][:, m, :])
